import numpy as np
import ml_dtypes


def mxq(x, axis, fmt="e4m3"):
    dtype, down = {"e4m3": (ml_dtypes.float8_e4m3fn, 7), "e5m2": (ml_dtypes.float8_e5m2, 14)}[fmt]
    v = np.moveaxis(np.asarray(x, np.float32).astype(ml_dtypes.bfloat16).astype(np.float64), axis, -1)
    blocks = v.reshape(v.shape[:-1] + (-1, 32))
    amax = np.abs(blocks).max(-1, keepdims=True)
    byte = np.maximum(np.where(amax > 0, np.frexp(amax)[1] - 1 + 127, 0) - down, 1)
    scale = np.exp2(byte - 127.0)
    codes = (blocks / scale).astype(np.float32).astype(dtype).astype(np.float64)
    return np.moveaxis((codes * scale).reshape(v.shape), -1, axis)


WIDE = False


def mx_kscale(k):
    if not WIDE:
        return np.ones(k)
    levels = np.array([10, -10, 5, -5, 0])
    if k % 512:
        return np.exp2(np.random.permutation(np.resize(levels, k // 32))).repeat(32)
    a = np.empty((k // 512, 16))
    for p in range(k // 512):
        a[p, :8] = np.random.permutation(np.resize(levels, 8))
        for g in range(8):
            far = levels[np.abs(levels - a[p, g]) >= 10]
            a[p, g + 8] = far[np.random.randint(len(far))]
    return np.exp2(a.ravel()).repeat(32)


def f64(x):
    return np.asarray(x).astype(np.float64)


def striped(idx):
    return np.tile(idx.reshape(-1, 16).T, (8, 1)).astype(np.uint16)


def unstriped(offs):
    return offs[:16].T.reshape(-1).astype(np.int64)


E2M1 = np.array([0.0, 0.5, 1.0, 1.5, 2.0, 3.0, 4.0, 6.0, -0.0, -0.5, -1.0, -1.5, -2.0, -3.0, -4.0, -6.0])


def pack_weight(w, fmt):
    k, n = w.shape
    w = f64(np.asarray(w, np.float32).astype(ml_dtypes.bfloat16)).reshape(k // 32, 32, n)
    amax = np.abs(w).max(1)
    if fmt == "e4m3":
        byte = np.frexp(amax)[1] - 1 + 127 - 7
    else:
        mant, ex = np.frexp(amax / 6.0)
        byte = np.where(mant > 0.5, ex, ex - 1) + 127
    byte = np.clip(np.where(amax > 0, byte, 1), 1, 254)
    scaled = (w * np.exp2(127.0 - byte)[:, None, :]).reshape(k, n).astype(np.float32)
    by_word = np.ascontiguousarray(scaled.reshape(k // 512, 128, 4, n).transpose(0, 1, 3, 2))
    if fmt == "e4m3":
        words = by_word.astype(ml_dtypes.float8_e4m3fn).view(np.uint8)
    else:
        c = by_word.astype(ml_dtypes.float4_e2m1fn).view(np.uint8) & 0xF
        words = (c[..., 0::2] | (c[..., 1::2] << 4)).reshape(k // 512, 128, 2 * n)
    return np.ascontiguousarray(words), np.ascontiguousarray(byte.astype(np.uint8).reshape(k // 512, 16, n))


def unpack_weight(words, scales, fmt):
    g, _, n = scales.shape
    words = np.ascontiguousarray(words).reshape(g, 128, n, -1)
    if fmt == "e4m3":
        vals = words.view(ml_dtypes.float8_e4m3fn).astype(np.float64)
    else:
        nib = np.empty((g, 128, n, 4), np.uint8)
        nib[..., 0::2] = words & 0xF
        nib[..., 1::2] = words >> 4
        vals = E2M1[nib]
    vals = vals * np.repeat(np.exp2(scales.astype(np.float64) - 127.0), 8, axis=1)[..., None]
    return vals.transpose(0, 1, 3, 2).reshape(g * 512, n)


def pack_table(v):
    words, scales = pack_weight(v, "e4m3")
    return np.concatenate([words.reshape(words.shape[0], -1), scales.reshape(scales.shape[0], -1)], axis=1)


def unpack_table(tab):
    g, t = tab.shape[0], tab.shape[1] // 528
    return unpack_weight(tab[:, :512 * t].reshape(g, 128, t, 4), tab[:, 512 * t:].reshape(g, 16, t), "e4m3")


def silu(v):
    return v / (1.0 + np.exp(-np.maximum(v, -700.0)))


K, M, T, S = 2048, 128, 2048, 512


def setup_inputs():
    n = np.random.standard_normal
    s = mx_kscale(K)[:, None]
    return {
        "tab": pack_table(n((K, T)) * s),
        "w": (n((K, M)) / np.sqrt(K) / s).astype(np.float32),
        "b": (0.3 * n(128)).astype(np.float32),
        "offs": striped(np.random.permutation(T)[:S]),
    }


def reference(tab, w, b, offs):
    tab_ = unpack_table(tab)[:, unstriped(offs)]
    w_ = mxq(f64(w), 0, "e4m3")
    y = w_.T @ tab_
    return silu(y + f64(b)[:, None])

@@ -1,0 +1,84 @@
+from contextlib import ExitStack
+
+import concourse.mybir as mybir
+
+K, M, T, S = 2048, 128, 2048, 512
+P = 128
+PASSES = 4
+HALF = 256
+FLOPS = 2 * K * M * S
+
+F32 = mybir.dt.float32
+BF16 = mybir.dt.bfloat16
+I32 = mybir.dt.int32
+U32 = mybir.dt.uint32
+U16 = mybir.dt.uint16
+U8 = mybir.dt.uint8
+FP8X4 = mybir.dt.float8_e4m3fn_x4
+SILU = mybir.ActivationFunctionType.Silu
+
+
+def tile_list_tabw_silu_kernel(tc, tab, w, b, offs, out):
+    nc = tc.nc
+    with ExitStack() as ctx:
+        held = ctx.enter_context(tc.tile_pool(name="held", bufs=1))
+        psum = ctx.enter_context(tc.psum_pool(name="psum", bufs=1))
+
+        offsets = held.tile([P, S // 16], U16, name="offsets")
+        packed = held.tile([P, T // 4], I32, name="packed", align_bytes=64)
+        bias = held.tile([P, 1], F32, name="bias")
+        warm = held.tile([P, 1], F32, name="warm")
+        warmed = held.tile([P, 1], F32, name="warmed")
+        words = [held.tile([P, T], I32, name=f"words{a}", align_bytes=64) for a in range(PASSES)]
+        picked = [held.tile([P, S], U32, name=f"picked{a}", align_bytes=64) for a in range(PASSES)]
+        picked_scales = held.tile([P, S], U8, name="picked_scales", align_bytes=64)
+        acc = [psum.tile([P, HALF], F32, name=f"acc{h}") for h in range(2)]
+        result = [held.tile([P, HALF], F32, name=f"result{h}", align_bytes=64) for h in range(2)]
+
+        raw = [held.tile([P, 4, M], F32, name=f"raw{a}", align_bytes=64) for a in range(PASSES)]
+        grouped = [held.tile([P, M, 4], BF16, name=f"grouped{a}", align_bytes=64) for a in range(PASSES)]
+        codes = [held.tile([P, M], U32, name=f"codes{a}", align_bytes=64) for a in range(PASSES)]
+        scales = [held.tile([P, M], U8, name=f"scales{a}", align_bytes=64) for a in range(PASSES)]
+
+        nc.vector.memset(packed[:], 0)
+        nc.vector.memset(warm[:], 0.0)
+        scale_rows = tab[:, 512 * T : 528 * T].bitcast(I32).rearrange("a (q t) -> a q t", q=16)
+        for quad in range(4):
+            nc.gpsimd.dma_start(packed[32 * quad : 32 * quad + 16, :], scale_rows[:, 4 * quad : 4 * quad + 4, :])
+        nc.sync.dma_start(offsets[:], offs)
+        for a in range(PASSES):
+            nc.sync.dma_start(words[a][:], tab[a, 0 : 512 * T].bitcast(I32).rearrange("(p t) -> p t", p=P))
+        for a in range(PASSES):
+            nc.sync.dma_start(raw[a][:], w[512 * a : 512 * (a + 1), :].rearrange("(p j) n -> p j n", j=4))
+        nc.scalar.dma_start(bias[:], b.rearrange("(p o) -> p o", o=1))
+        nc.scalar.activation(warmed[:], warm[:], SILU)
+
+        def multiply(a, h):
+            cols = slice(h * HALF, (h + 1) * HALF)
+            nc.tensor.matmul_mx(
+                out=acc[h][:],
+                lhsT=codes[a][:].bitcast(FP8X4),
+                lhsT_scale=scales[a][:],
+                rhs=picked[a][:, cols].bitcast(FP8X4),
+                rhs_scale=picked_scales[4 * a :, cols],
+                start=(a == 0),
+                stop=(a == PASSES - 1),
+            )
+
+        for a in range(PASSES):
+            nc.vector.tensor_copy(picked[a][:], words[a][:].bitcast(U32).indirect(offsets[:]))
+            if a == 0:
+                nc.vector.tensor_copy(picked_scales[:], packed[:].bitcast(U8).indirect(offsets[:]))
+        for a in range(PASSES):
+            src, dst = raw[a][:].rearrange("p j n -> p n j"), grouped[a][:]
+            if a in (0, 1, 2):
+                nc.scalar.copy(dst, src)
+            else:
+                nc.vector.tensor_copy(dst, src)
+            nc.vector.quantize_mx(out=codes[a][:].bitcast(FP8X4), scales=scales[a][:], in_=grouped[a][:].rearrange("p n j -> p (n j)"))
+            for h in range(2):
+                multiply(a, h)
+
+        for h, queue in enumerate((nc.sync, nc.scalar)):
+            nc.scalar.activation(result[h][:], acc[h][:], SILU, bias=bias[:])
+            queue.dma_start(out[:, h * HALF : (h + 1) * HALF], result[h][:])

@@ -44,7 +44,7 @@ def tile_list_tabw_silu_kernel(tc, tab, w, b, offs, out):
         nc.vector.memset(warm[:], 0.0)
         scale_rows = tab[:, 512 * T : 528 * T].bitcast(I32).rearrange("a (q t) -> a q t", q=16)
         for quad in range(4):
-            nc.gpsimd.dma_start(packed[32 * quad : 32 * quad + 16, :], scale_rows[:, 4 * quad : 4 * quad + 4, :])
+            nc.scalar.dma_start(packed[32 * quad : 32 * quad + 16, :], scale_rows[:, 4 * quad : 4 * quad + 4, :])
         nc.sync.dma_start(offsets[:], offs)
         for a in range(PASSES):
             nc.sync.dma_start(words[a][:], tab[a, 0 : 512 * T].bitcast(I32).rearrange("(p t) -> p t", p=P))

@@ -50,7 +50,7 @@ def tile_list_tabw_silu_kernel(tc, tab, w, b, offs, out):
             nc.sync.dma_start(words[a][:], tab[a, 0 : 512 * T].bitcast(I32).rearrange("(p t) -> p t", p=P))
         for a in range(PASSES):
             nc.sync.dma_start(raw[a][:], w[512 * a : 512 * (a + 1), :].rearrange("(p j) n -> p j n", j=4))
-        nc.scalar.dma_start(bias[:], b.rearrange("(p o) -> p o", o=1))
+        nc.sync.dma_start(bias[:], b.rearrange("(p o) -> p o", o=1))
         nc.scalar.activation(warmed[:], warm[:], SILU)
 
         def multiply(a, h):
@@ -79,6 +79,6 @@ def tile_list_tabw_silu_kernel(tc, tab, w, b, offs, out):
             for h in range(2):
                 multiply(a, h)
 
-        for h, queue in enumerate((nc.sync, nc.scalar)):
+        for h in range(2):
             nc.scalar.activation(result[h][:], acc[h][:], SILU, bias=bias[:])
-            queue.dma_start(out[:, h * HALF : (h + 1) * HALF], result[h][:])
+            nc.sync.dma_start(out[:, h * HALF : (h + 1) * HALF], result[h][:])

from contextlib import ExitStack

import concourse.mybir as mybir

K, M, T, S = 2048, 128, 2048, 512
P = 128
PASSES = 4
HALF = 256
FLOPS = 2 * K * M * S

F32 = mybir.dt.float32
BF16 = mybir.dt.bfloat16
I32 = mybir.dt.int32
U32 = mybir.dt.uint32
U16 = mybir.dt.uint16
U8 = mybir.dt.uint8
FP8X4 = mybir.dt.float8_e4m3fn_x4
SILU = mybir.ActivationFunctionType.Silu


def tile_list_tabw_silu_kernel(tc, tab, w, b, offs, out):
    nc = tc.nc
    with ExitStack() as ctx:
        held = ctx.enter_context(tc.tile_pool(name="held", bufs=1))
        psum = ctx.enter_context(tc.psum_pool(name="psum", bufs=1))

        offsets = held.tile([P, S // 16], U16, name="offsets")
        packed = held.tile([P, T // 4], I32, name="packed", align_bytes=64)
        bias = held.tile([P, 1], F32, name="bias")
        warm = held.tile([P, 1], F32, name="warm")
        warmed = held.tile([P, 1], F32, name="warmed")
        words = [held.tile([P, T], I32, name=f"words{a}", align_bytes=64) for a in range(PASSES)]
        picked = [held.tile([P, S], U32, name=f"picked{a}", align_bytes=64) for a in range(PASSES)]
        picked_scales = held.tile([P, S], U8, name="picked_scales", align_bytes=64)
        acc = [psum.tile([P, HALF], F32, name=f"acc{h}") for h in range(2)]
        result = [held.tile([P, HALF], F32, name=f"result{h}", align_bytes=64) for h in range(2)]

        raw = [held.tile([P, 4, M], F32, name=f"raw{a}", align_bytes=64) for a in range(PASSES)]
        grouped = [held.tile([P, M, 4], BF16, name=f"grouped{a}", align_bytes=64) for a in range(PASSES)]
        codes = [held.tile([P, M], U32, name=f"codes{a}", align_bytes=64) for a in range(PASSES)]
        scales = [held.tile([P, M], U8, name=f"scales{a}", align_bytes=64) for a in range(PASSES)]

        nc.vector.memset(packed[:], 0)
        nc.vector.memset(warm[:], 0.0)
        scale_rows = tab[:, 512 * T : 528 * T].bitcast(I32).rearrange("a (q t) -> a q t", q=16)
        for quad in range(4):
            nc.scalar.dma_start(packed[32 * quad : 32 * quad + 16, :], scale_rows[:, 4 * quad : 4 * quad + 4, :])
        nc.sync.dma_start(offsets[:], offs)
        for a in range(PASSES):
            nc.sync.dma_start(words[a][:], tab[a, 0 : 512 * T].bitcast(I32).rearrange("(p t) -> p t", p=P))
        for a in range(PASSES):
            nc.sync.dma_start(raw[a][:], w[512 * a : 512 * (a + 1), :].rearrange("(p j) n -> p j n", j=4))
        nc.sync.dma_start(bias[:], b.rearrange("(p o) -> p o", o=1))
        nc.scalar.activation(warmed[:], warm[:], SILU)

        def multiply(a, h):
            cols = slice(h * HALF, (h + 1) * HALF)
            nc.tensor.matmul_mx(
                out=acc[h][:],
                lhsT=codes[a][:].bitcast(FP8X4),
                lhsT_scale=scales[a][:],
                rhs=picked[a][:, cols].bitcast(FP8X4),
                rhs_scale=picked_scales[4 * a :, cols],
                start=(a == 0),
                stop=(a == PASSES - 1),
            )

        for a in range(PASSES):
            nc.vector.tensor_copy(picked[a][:], words[a][:].bitcast(U32).indirect(offsets[:]))
            if a == 0:
                nc.vector.tensor_copy(picked_scales[:], packed[:].bitcast(U8).indirect(offsets[:]))
        for a in range(PASSES):
            src, dst = raw[a][:].rearrange("p j n -> p n j"), grouped[a][:]
            if a in (0, 1, 2):
                nc.scalar.copy(dst, src)
            else:
                nc.vector.tensor_copy(dst, src)
            nc.vector.quantize_mx(out=codes[a][:].bitcast(FP8X4), scales=scales[a][:], in_=grouped[a][:].rearrange("p n j -> p (n j)"))
            for h in range(2):
                multiply(a, h)

        for h in range(2):
            nc.scalar.activation(result[h][:], acc[h][:], SILU, bias=bias[:])
            nc.sync.dma_start(out[:, h * HALF : (h + 1) * HALF], result[h][:])
